import numpy as np, ml_dtypes
CORES = [12,28,44,60,3,19,35,51]
N = 8
def setup_inputs(rng):
    m = (rng.standard_normal((N, 128, 128), dtype=np.float32) / 11).astype(ml_dtypes.bfloat16)
    return {"m": m, "mt": m.transpose(0, 2, 1).copy()}
def setup_inputs_low(rng):
    d = setup_inputs(rng)
    for k in ("m", "mt"): d[k] = (d[k].astype(np.float32) * 0.125).astype(d[k].dtype)
    return d
def reference(m, mt):
    M = m.astype(np.float64); p = M[0]
    for r in range(1, N):
        p = p @ M[r]
    p = p.astype(ml_dtypes.bfloat16)
    return {"y": np.broadcast_to(p, (N, 128, 128))}

from concourse.bass import DstId, RemoteDMATransfer

W = 128
SIM_CORES = 64
RELAY_ENGINES = 8

SCRATCH = {
    "gat": ("sbuf", [128, 8 * W], "bfloat16"),
    "stage": ("dram", [128, W], "bfloat16"),
    "pairA": ("sbuf", [128, 2 * W], "bfloat16"),
    "pairB": ("sbuf", [128, 2 * W], "bfloat16"),
    "halfA": ("sbuf", [128, W], "bfloat16"),
    "halfB": ("sbuf", [128, W], "bfloat16"),
    "ysb": ("sbuf", [128, W], "bfloat16"),
    "psXA": ("psum", [128, 512], "float32"),
    "psYA": ("psum", [128, 512], "float32"),
    "psHA": ("psum", [128, 512], "float32"),
    "psXB": ("psum", [128, 512], "float32"),
    "psYB": ("psum", [128, 512], "float32"),
    "psHB": ("psum", [128, 512], "float32"),
    "psF": ("psum", [128, 512], "float32"),
}
SEMAPHORES = (["ld_s", "ld_d", "rel", "sent", "prod", "mf", "cf", "st"]
              + ["a%d" % r for r in range(8)]
              + [k + t for t in "AB" for k in ("mx", "my", "cx", "cy", "mh", "ch")])


def _count(mask):
    return sum(1 for b in range(mask.bit_length()) if (mask >> b) & 1)


def _first(mask, n):
    bits = [b for b in range(mask.bit_length()) if (mask >> b) & 1]
    return sum(1 << b for b in bits[:n])


def _common_mask(topo, src, dsts):
    m = topo.mask(src, dsts[0])
    for d in dsts[1:]:
        m &= topo.mask(src, d)
    return m


def _mate_index(topo, c, other):
    return [j for j, d in enumerate(other) if topo.mates(topo.chip(c), topo.chip(d))][0]


def _plan(T, topo):
    cores = list(T.cores)
    h = len(cores) // 2
    halves = (cores[:h], cores[h:])
    direct = []
    partner = {}
    relays = {}
    job = {}
    for side in (0, 1):
        own, other = halves[side], halves[1 - side]
        ok = all(topo.may_write(c, d) for c in own for d in other)
        direct.append(ok)
        for c in own:
            j0 = _mate_index(topo, c, other)
            if ok:
                partner[c] = other[j0]
                continue
            cand = [x for x in range(SIM_CORES)
                    if topo.chip(x) == topo.chip(c) and x not in cores
                    and all(topo.may_write(x, d) for d in other)]
            cand.sort(key=lambda x: (topo.die(x) != topo.die(other[j0]), x))
            for j, d in enumerate(other):
                x = cand[((j - j0) % h) % len(cand)]
                job.setdefault(x, (cores.index(c), []))[1].append(d)
            same = [x for x in cand if topo.die(x) == topo.die(other[j0])]
            far = [x for x in cand if x not in same]
            mixed = []
            for a, b in zip(far, reversed(same)):
                mixed += [a, b]
            mixed = [x for x in cand if x not in mixed] + mixed
            relays[c] = [x for x in mixed if x in job]
    return halves, direct, partner, relays, job


def _slot(T, r):
    return T.gat[:, r * W:(r + 1) * W]


def _send(g, T, topo, src, dst_ap, dsts, mask, remote_sem):
    ids = []
    for d in dsts:
        rid, pid, _se = topo.addr(d)
        ids.append(DstId(rid=rid, pnc=pid))
    g.remote_dma_fused(
        [RemoteDMATransfer(dst_ids=ids, dma_engine_mask=mask, remote_sem=remote_sem,
                           srcs=[src], dsts=[dst_ap for _d in dsts], alu_op=0)],
        local_sem=T.sem.sent)
    return _count(mask)


def _half_product(g, T, tag, base, left, ready, y_first, out):
    te, ve, S = g.tensor, g.vector, T.sem
    pair = T["pair" + tag]
    X, Y = pair[:, 0:W], pair[:, W:2 * W]
    psx, psy, psh = T["psX" + tag][:, 0:W], T["psY" + tag][:, 0:W], T["psH" + tag][:, 0:W]
    steps = [("x", psx, X, 1, 0), ("y", psy, Y, 2, 3)]
    if y_first:
        steps.reverse()
    for k, ps, _sb, a, b in steps:
        for q in (a, b):
            te.wait_ge(ready[q][0], ready[q][1])
        te.matmul(ps, _slot(T, base + a), _slot(T, base + b), True, True).then_inc(S["m" + k + tag], 1)
    for k, ps, sb, _a, _b in steps:
        ve.wait_ge(S["m" + k + tag], 1)
        ve.tensor_copy(sb, ps).then_inc(S["c" + k + tag], 1)
    te.wait_ge(S["cx" + tag], 1)
    te.wait_ge(S["cy" + tag], 1)
    if left:
        te.matmul(psh, Y, X, True, True).then_inc(S["mh" + tag], 1)
    else:
        te.matmul(psh, X, Y, True, True).then_inc(S["mh" + tag], 1)
    ve.wait_ge(S["mh" + tag], 1)
    ve.tensor_copy(out, psh).then_inc(S["ch" + tag], 1)


def rank_program(g, core, T, topo):
    halves, direct, partner, relays, job = _plan(T, topo)
    S = T.sem
    rank = T.rank_of(core)

    if rank is None:
        if core not in job:
            return
        slot, dsts = job[core]
        g.wait_ge(S.rel, RELAY_ENGINES)
        n = _send(g, T, topo, T.stage[:], _slot(T, slot), dsts, _common_mask(topo, core, dsts), S["a%d" % slot])
        g.wait_ge(S.sent, n)
        return

    h = len(halves[0])
    side = 0 if core in halves[0] else 1
    own, other = halves[side], halves[1 - side]
    base, obase = side * h, (1 - side) * h
    i = rank - base
    form = T.mt if rank % 2 == 0 else T.m
    mine = _slot(T, rank)
    sent = 0

    g.sync.dma_start(mine, form[:]).then_inc(S.ld_s, 16)
    if not direct[side]:
        g.scalar.dma_start(T.stage[:], form[:]).then_inc(S.ld_d, 16)
        g.wait_ge(S.ld_d, 16)
        rl = relays[core]
        sent += _send(g, T, topo, T.stage[:], T.stage[:], rl,
                      _first(_common_mask(topo, core, rl), RELAY_ENGINES), S.rel)
    peers = [own[i ^ k] for k in range(1, h)]
    g.wait_ge(S.ld_s, 16)
    sent += _send(g, T, topo, mine, mine, peers, _common_mask(topo, core, peers), S["a%d" % rank])

    ready = [(S.ld_s, 16) if k == i else (S["a%d" % (base + k)], _count(topo.mask(own[k], core))) for k in range(h)]
    _half_product(g, T, "A", base, side == 0, ready, i >= h // 2, T.halfA[:])

    if direct[side]:
        d = partner[core]
        g.wait_ge(S.chA, 1)
        sent += _send(g, T, topo, T.halfA[:], T.halfB[:], [d], topo.mask(core, d), S.prod)

    if direct[1 - side]:
        src = [c for c in other if partner[c] == core][0]
        g.tensor.wait_ge(S.prod, _count(topo.mask(src, core)))
    else:
        oready = []
        for k in range(h):
            x = [r for r in job if job[r][0] == obase + k and core in job[r][1]][0]
            oready.append((S["a%d" % (obase + k)], _count(_common_mask(topo, x, job[x][1]))))
        _half_product(g, T, "B", obase, side == 1, oready, _mate_index(topo, core, other) < h // 2, T.halfB[:])
        g.tensor.wait_ge(S.chB, 1)
    g.tensor.wait_ge(S.chA, 1)

    lt, r = (T.halfA[:], T.halfB[:]) if side == 0 else (T.halfB[:], T.halfA[:])
    g.tensor.matmul(T.psF[:, 0:W], lt, r, True, True).then_inc(S.mf, 1)
    g.vector.wait_ge(S.mf, 1)
    g.vector.tensor_copy(T.ysb[:], T.psF[:, 0:W]).then_inc(S.cf, 1)
    g.sync.wait_ge(S.cf, 1)
    g.sync.dma_start(T.y[:], T.ysb[:]).then_inc(S.st, 16)
    g.sync.wait_ge(S.st, 16)
    g.wait_ge(S.sent, sent)
